import numpy as np
import ml_dtypes


def mxq(x, axis, fmt="e4m3"):
    dtype, down = {"e4m3": (ml_dtypes.float8_e4m3fn, 7), "e5m2": (ml_dtypes.float8_e5m2, 14)}[fmt]
    v = np.moveaxis(np.asarray(x, np.float32).astype(ml_dtypes.bfloat16).astype(np.float64), axis, -1)
    blocks = v.reshape(v.shape[:-1] + (-1, 32))
    amax = np.abs(blocks).max(-1, keepdims=True)
    byte = np.maximum(np.where(amax > 0, np.frexp(amax)[1] - 1 + 127, 0) - down, 1)
    scale = np.exp2(byte - 127.0)
    codes = (blocks / scale).astype(np.float32).astype(dtype).astype(np.float64)
    return np.moveaxis((codes * scale).reshape(v.shape), -1, axis)


WIDE = False


def mx_kscale(k):
    if not WIDE:
        return np.ones(k)
    levels = np.array([10, -10, 5, -5, 0])
    if k % 512:
        return np.exp2(np.random.permutation(np.resize(levels, k // 32))).repeat(32)
    a = np.empty((k // 512, 16))
    for p in range(k // 512):
        a[p, :8] = np.random.permutation(np.resize(levels, 8))
        for g in range(8):
            far = levels[np.abs(levels - a[p, g]) >= 10]
            a[p, g + 8] = far[np.random.randint(len(far))]
    return np.exp2(a.ravel()).repeat(32)


def f64(x):
    return np.asarray(x).astype(np.float64)


def striped(idx):
    return np.tile(idx.reshape(-1, 16).T, (8, 1)).astype(np.uint16)


def unstriped(offs):
    return offs[:16].T.reshape(-1).astype(np.int64)


def striped8(idx):
    return np.concatenate([x.reshape(-1, 16).T for x in idx]).astype(np.uint16)


def runs(offs, k):
    lists = np.stack([offs[16 * r : 16 * r + 16].T.reshape(-1) for r in range(8)]).astype(np.int64)
    return lists[np.arange(k) % 512 // 64]


def pack_weight(w):
    k, n = w.shape
    w = f64(np.asarray(w, np.float32).astype(ml_dtypes.bfloat16)).reshape(k // 32, 32, n)
    amax = np.abs(w).max(1)
    byte = np.clip(np.where(amax > 0, np.frexp(amax)[1] - 1 + 127 - 7, 1), 1, 254)
    scaled = (w * np.exp2(127.0 - byte)[:, None, :]).reshape(k, n).astype(np.float32)
    words = np.ascontiguousarray(scaled.reshape(k // 512, 128, 4, n).transpose(0, 1, 3, 2)).astype(ml_dtypes.float8_e4m3fn).view(np.uint8)
    return words, np.ascontiguousarray(byte.astype(np.uint8).reshape(k // 512, 16, n))


def unpack_weight(words, scales):
    g, p, n, _ = words.shape
    vals = np.ascontiguousarray(words).view(ml_dtypes.float8_e4m3fn).astype(np.float64) * np.repeat(np.exp2(scales.astype(np.float64) - 127.0), 8, axis=1)[..., None]
    return vals.transpose(0, 1, 3, 2).reshape(g * 512, n)

def planes(y):
    n, m = y.shape
    v = y.astype(np.float32).astype(ml_dtypes.bfloat16).astype(np.float64).reshape(n // 32, 32, m)
    top = np.abs(v).max(1)
    byte = np.clip(np.where(top > 0, np.frexp(top)[1] - 1 + 127 - 7, 1), 1, 254)
    codes = (v * np.exp2(127.0 - byte)[:, None, :]).reshape(n, m).astype(np.float32).astype(ml_dtypes.float8_e4m3fn).view(np.uint8)
    words = codes.reshape(n // 512, 128, 4, m).transpose(0, 1, 3, 2)
    return np.ascontiguousarray(words), np.ascontiguousarray(byte.astype(np.uint8).reshape(n // 512, 16, m))


K, T, S, G, H, W, U = 512, 1024, 256, 2048, 512, 128, 512


def setup_inputs():
    n = np.random.standard_normal
    s = mx_kscale(K)[:, None]
    packed_xT = pack_weight(n((K, T)) * s)
    packed_dT = pack_weight(n((K, G)) / s)
    perm = np.random.permutation(S)
    perm2 = np.random.permutation(U)
    return {
        "x_words": packed_xT[0],
        "x_scales": packed_xT[1],
        "d_words": packed_dT[0],
        "d_scales": packed_dT[1],
        "gs": (np.random.uniform(0.5, 1.5, (K, 1)) * s).astype(np.float32),
        "offs": striped8(np.random.randint(0, T, (8, S))),
        "k1": striped8(np.random.randint(0, G, (8, H))),
        "n1": striped(perm[:W]),
        "n2": striped(perm[W:]),
        "n3": striped(np.random.permutation(S)),
        "k2": striped8(np.random.randint(0, G, (8, H))),
        "n4": striped(perm2[:S]),
        "n5": striped(perm2[S:]),
        "n6": striped(np.random.permutation(S)),
    }


def reference(x_words, x_scales, d_words, d_scales, gs, offs, k1, n1, n2, n3, k2, n4, n5, n6):
    d_k2 = unpack_weight(d_words, d_scales)[np.arange(K)[:, None], runs(k2, K)]
    d_k1 = unpack_weight(d_words, d_scales)[np.arange(K)[:, None], runs(k1, K)]
    xq = unpack_weight(x_words, x_scales)[np.arange(K)[:, None], runs(offs, K)]
    h = 0.0625 * (d_k1.T @ xq)
    pa = h[:, unstriped(n1)]
    pb = h[:, unstriped(n2)]
    rb = pa - pb
    ds = np.zeros((H, S))
    ds[:, unstriped(n1)] = pb
    dt = ds.copy()
    dt[:, unstriped(n2)] = rb
    z = f64(gs) * (np.maximum(dt, 0.5 * dt[:, unstriped(n3)]))
    h2 = 0.0625 * ((d_k2.T @ mxq(z, 0, "e4m3")))
    dn = np.minimum(h2, h2[:, unstriped(n6)])
    up = np.maximum(h2, h2[:, unstriped(n6)])
    ph = np.zeros((H, U))
    ph[:, unstriped(n4)] = up
    out = ph.copy()
    out[:, unstriped(n5)] = dn
    return (out,) + planes(out)

@@ -1,0 +1,223 @@
+from contextlib import ExitStack
+
+import concourse.mybir as mybir
+
+K, T, S, G, H, W, U = 512, 1024, 256, 2048, 512, 128, 512
+FLOPS = 2 * 2 * K * H * S
+
+F32 = mybir.dt.float32
+BF16 = mybir.dt.bfloat16
+I32 = mybir.dt.int32
+U32 = mybir.dt.uint32
+U16 = mybir.dt.uint16
+U8 = mybir.dt.uint8
+FP8X4 = mybir.dt.float8_e4m3fn_x4
+ALU = mybir.AluOpType
+COPY = mybir.ActivationFunctionType.Copy
+
+P = 128
+PACK = 4
+HALF = S // 2
+LIST_COLS = HALF // 16
+
+
+def tile_picked_hcodeswapdpagmx_none_po_kernel(
+    tc, x_words, x_scales, d_words, d_scales, gs, offs, k1, n1, n2, n3, k2, n4, n5, n6, out_0, out_1, out_2
+):
+    nc = tc.nc
+    with ExitStack() as ctx:
+        sb = ctx.enter_context(tc.tile_pool(name="sb", bufs=1))
+        psum = ctx.enter_context(tc.psum_pool(name="psum", bufs=1))
+
+        def tile(name, shape, dtype, tag=None):
+            return sb.tile(shape, dtype, name=name, tag=tag or name, align_bytes=64)
+
+        def load_list(name, src):
+            t = sb.tile(list(src.shape), U16, name=name)
+            nc.sync.dma_start(t[:], src)
+            return t
+
+        def load_scale_rows(name, src, width):
+            t = tile(name, [P, width], U8)
+            rows = src[0].bitcast(I32).unsqueeze(1).to_broadcast([16, 8, width // 4])
+            nc.sync.dma_start(t[:].bitcast(I32), rows)
+            return t
+
+        def load_words(name, src, width):
+            t = tile(name, [P, width], U32)
+            nc.sync.dma_start(t[:].bitcast(I32), src[0].rearrange("p n t -> p (n t)").bitcast(I32))
+            return t
+
+        def place_odd_rows(plane, queues):
+            for r in range(1, 4):
+                queues[r - 1].dma_start(plane[r:P:32, :].bitcast(I32), plane[8 * r : P : 32, :].bitcast(I32))
+
+        def deal(dst, src):
+            nc.vector.tensor_copy(dst.rearrange("p (t m) -> p t m", t=PACK), src.rearrange("p (m t) -> p t m", t=PACK))
+
+        d_sc = load_scale_rows("d_sc", d_scales, G)
+        k1_t = load_list("k1_t", k1)
+        x_sc = load_scale_rows("x_sc", x_scales, T)
+        offs_t = load_list("offs_t", offs)
+        d_w = load_words("d_w", d_words, G)
+        x_w = load_words("x_w", x_words, T)
+        n2_t = load_list("n2_t", n2)
+        n1_t = load_list("n1_t", n1)
+
+        k1_sc_g = tile("k1_sc_g", [P, H], U8)
+        x_sc_g = tile("x_sc_g", [P, S], U8)
+        nc.vector.tensor_copy(k1_sc_g[:], d_sc[:].indirect(k1_t[:]))
+        nc.vector.tensor_copy(x_sc_g[:], x_sc[:].indirect(offs_t[:]))
+        plane1 = tile("plane1", [P, H + S], U8)
+        deal(plane1[:, :H], k1_sc_g[:])
+        nc.vector.tensor_copy(plane1[:, H:].bitcast(I32), x_sc_g[:].bitcast(I32))
+        place_odd_rows(plane1, [nc.scalar, nc.scalar, nc.scalar])
+
+        k1_w_g = tile("k1_w_g", [P, H], U32)
+        xq = tile("xq", [P, S], U32, tag="xq")
+        nc.vector.tensor_copy(k1_w_g[:], d_w[:].indirect(k1_t[:]))
+        nc.vector.tensor_copy(xq[:], x_w[:].indirect(offs_t[:]))
+        w1 = tile("w1", [P, H], U32)
+        deal(w1[:].bitcast(I32), k1_w_g[:].bitcast(I32))
+
+        n3_t = load_list("n3_t", n3)
+        gs_t = tile("gs_t", [P, PACK], F32)
+        nc.sync.dma_start(gs_t[:], gs.rearrange("(p t) o -> p (t o)", t=PACK))
+        k2_t = load_list("k2_t", k2)
+        n6_t = load_list("n6_t", n6)
+        n4_t = load_list("n4_t", n4)
+        n5_t = load_list("n5_t", n5)
+
+        h = []
+        for t in range(PACK):
+            acc = psum.tile([P, S], F32, name=f"acc{t}", tag=f"bank{t}")
+            cols = slice(t * P, (t + 1) * P)
+            nc.tensor.matmul_mx(
+                out=acc[:], lhsT=w1[:, cols].bitcast(FP8X4), lhsT_scale=plane1[:, cols],
+                rhs=xq[:].bitcast(FP8X4), rhs_scale=plane1[:, H:], start=True, stop=True,
+            )
+            ht = tile(f"h{t}", [P, S], F32)
+            nc.vector.tensor_scalar(ht[:], acc[:], 0.0625, None, ALU.mult)
+            h.append(ht)
+
+        pa = [tile(f"pa{t}", [P, W], F32) for t in range(PACK)]
+        pb = [tile(f"pb{t}", [P, W], F32) for t in range(PACK)]
+        rb = [tile(f"rb{t}", [P, W], F32) for t in range(PACK)]
+        dt = [tile(f"dt{t}", [P, S], F32) for t in range(PACK)]
+        zb = [tile(f"zb{a}", [P, HALF, PACK], BF16) for a in range(2)]
+
+        def fetch_pair(t):
+            nc.scalar.activation(pb[t][:], h[t][:].indirect(n2_t[:]), COPY)
+            nc.scalar.activation(pa[t][:], h[t][:].indirect(n1_t[:]), COPY)
+            nc.vector.tensor_tensor(rb[t][:], pa[t][:], pb[t][:], ALU.subtract)
+
+        def put_pb(t):
+            nc.scalar.activation(dt[t][:].indirect(n1_t[:]), pb[t][:], COPY)
+
+        def put_rb(t):
+            nc.scalar.activation(dt[t][:].indirect(n2_t[:]), rb[t][:], COPY)
+
+        def make_z(t, a):
+            cols = slice(a * HALF, (a + 1) * HALF)
+            g = tile(f"g3_{t}_{a}", [P, HALF], F32)
+            m = tile(f"m_{t}_{a}", [P, HALF], F32)
+            nc.scalar.activation(g[:], dt[t][:].indirect(n3_t[:, a * LIST_COLS : (a + 1) * LIST_COLS]), COPY)
+            nc.vector.scalar_tensor_tensor(m[:], g[:], 0.5, dt[t][:, cols], ALU.mult, ALU.max)
+            nc.vector.tensor_scalar(zb[a][:, :, t], m[:], gs_t[:, t : t + 1], None, ALU.mult)
+
+        fetch_pair(0)
+        fetch_pair(1)
+        put_pb(0)
+        put_pb(1)
+        put_rb(0)
+        put_rb(1)
+
+        k2_sc_g = tile("k2_sc_g", [P, H], U8, tag="pa0")
+        nc.vector.tensor_copy(k2_sc_g[:], d_sc[:].indirect(k2_t[:]))
+        plane2 = tile("plane2", [P, H], U8)
+        deal(plane2[:], k2_sc_g[:])
+        place_odd_rows(plane2, [nc.sync, nc.sync, nc.sync])
+        k2_w_g = tile("k2_w_g", [P, H], U32, tag="rb0")
+        nc.vector.tensor_copy(k2_w_g[:], d_w[:].indirect(k2_t[:]))
+        w2 = tile("w2", [P, H], U32)
+        deal(w2[:].bitcast(I32), k2_w_g[:].bitcast(I32))
+
+        fetch_pair(2)
+        fetch_pair(3)
+        make_z(0, 0)
+        make_z(0, 1)
+        put_pb(2)
+        put_pb(3)
+        make_z(1, 0)
+        put_rb(2)
+        put_rb(3)
+        make_z(2, 0)
+        make_z(2, 1)
+        make_z(1, 1)
+        make_z(3, 0)
+        make_z(3, 1)
+
+        h2 = [tile(f"h2_{t}", [P, S], F32) for t in range(PACK)]
+        zq = []
+        for a in range(2):
+            codes = tile(f"zq{a}", [P, HALF], U32)
+            plane = tile(f"zs{a}", [P, HALF], U8)
+            nc.vector.quantize_mx(out=codes[:].bitcast(FP8X4), scales=plane[:], in_=zb[a][:].rearrange("p n t -> p (n t)"))
+            zq.append((codes, plane))
+        for t in range(PACK):
+            for a in range(2):
+                acc = psum.tile([P, HALF], F32, name=f"acc2_{t}_{a}", tag=f"bank{(t + PACK * (1 - a))}")
+                cols = slice(t * P, (t + 1) * P)
+                nc.tensor.matmul_mx(
+                    out=acc[:], lhsT=w2[:, cols].bitcast(FP8X4), lhsT_scale=plane2[:, cols],
+                    rhs=zq[a][0][:].bitcast(FP8X4), rhs_scale=zq[a][1][:], start=True, stop=True,
+                )
+                nc.vector.tensor_scalar(h2[t][:, a * HALF : (a + 1) * HALF], acc[:], 0.0625, None, ALU.mult)
+
+        up = [tile(f"up{t}", [P, S], F32) for t in range(PACK)]
+        dn = [tile(f"dn{t}", [P, S], F32) for t in range(PACK)]
+        page = [tile(f"page{t}", [P, U], F32) for t in range(PACK)]
+        ob = [tile(f"ob{a}", [P, U // 2, PACK], BF16) for a in range(2)]
+        out_rows = out_0.rearrange("(p t) c -> p t c", t=PACK)
+
+        def fetch_other(t):
+            g = tile(f"g6_{t}", [P, S], F32)
+            for a in range(2):
+                nc.scalar.activation(
+                    g[:, a * HALF : (a + 1) * HALF], h2[t][:].indirect(n6_t[:, a * LIST_COLS : (a + 1) * LIST_COLS]), COPY
+                )
+            nc.vector.tensor_tensor(up[t][:], h2[t][:], g[:], ALU.max)
+            nc.vector.tensor_tensor(dn[t][:], h2[t][:], g[:], ALU.min)
+
+        def put_up(t):
+            nc.scalar.activation(page[t][:].indirect(n4_t[:]), up[t][:], COPY)
+
+        def put_dn(t):
+            nc.scalar.activation(page[t][:].indirect(n5_t[:]), dn[t][:], COPY)
+            nc.sync.dma_start(out_rows[:, t, :], page[t][:])
+            for a in range(2):
+                nc.vector.tensor_copy(ob[a][:, :, t], page[t][:, a * (U // 2) : (a + 1) * (U // 2)])
+
+        fetch_other(0)
+        fetch_other(1)
+        put_up(0)
+        fetch_other(2)
+        put_dn(0)
+        put_up(1)
+        fetch_other(3)
+        put_dn(1)
+        put_up(2)
+        put_up(3)
+        put_dn(2)
+        put_dn(3)
+
+        o_plane = tile("o_plane", [P, U], U8)
+        words_out = out_1[0].rearrange("p n t -> p (n t)").bitcast(I32)
+        for a in range(2):
+            cols = slice(a * (U // 2), (a + 1) * (U // 2))
+            codes = tile(f"oq{a}", [P, U // 2], U32)
+            nc.vector.quantize_mx(out=codes[:].bitcast(FP8X4), scales=o_plane[:, cols], in_=ob[a][:].rearrange("p n t -> p (n t)"))
+            nc.sync.dma_start(words_out[:, cols], codes[:].bitcast(I32))
+        for q in range(4):
+            queue = nc.scalar if q % 2 == 0 else nc.sync
+            queue.dma_start(out_2[0, 4 * q : 4 * q + 4, :].bitcast(I32), o_plane[32 * q : 32 * q + 4, :].bitcast(I32))

@@ -52,37 +52,42 @@ def tile_picked_hcodeswapdpagmx_none_po_kernel(
             for r in range(1, 4):
                 queues[r - 1].dma_start(plane[r:P:32, :].bitcast(I32), plane[8 * r : P : 32, :].bitcast(I32))
 
+        def deal_words(dst, src):
+            nc.vector.tensor_copy(
+                dst.bitcast(I32).rearrange("p (t m) -> p m t", t=PACK), src.bitcast(I32).rearrange("p (m t) -> p m t", t=PACK)
+            )
+
         def deal(dst, src):
             nc.vector.tensor_copy(dst.rearrange("p (t m) -> p t m", t=PACK), src.rearrange("p (m t) -> p t m", t=PACK))
 
-        d_sc = load_scale_rows("d_sc", d_scales, G)
-        k1_t = load_list("k1_t", k1)
         x_sc = load_scale_rows("x_sc", x_scales, T)
         offs_t = load_list("offs_t", offs)
+        d_sc = load_scale_rows("d_sc", d_scales, G)
+        k1_t = load_list("k1_t", k1)
         d_w = load_words("d_w", d_words, G)
-        x_w = load_words("x_w", x_words, T)
         n2_t = load_list("n2_t", n2)
         n1_t = load_list("n1_t", n1)
+        n3_t = load_list("n3_t", n3)
+        x_w = load_words("x_w", x_words, T)
 
         k1_sc_g = tile("k1_sc_g", [P, H], U8)
         x_sc_g = tile("x_sc_g", [P, S], U8)
-        nc.vector.tensor_copy(k1_sc_g[:], d_sc[:].indirect(k1_t[:]))
         nc.vector.tensor_copy(x_sc_g[:], x_sc[:].indirect(offs_t[:]))
+        nc.vector.tensor_copy(k1_sc_g[:], d_sc[:].indirect(k1_t[:]))
         plane1 = tile("plane1", [P, H + S], U8)
-        deal(plane1[:, :H], k1_sc_g[:])
         nc.vector.tensor_copy(plane1[:, H:].bitcast(I32), x_sc_g[:].bitcast(I32))
-        place_odd_rows(plane1, [nc.scalar, nc.scalar, nc.scalar])
+        deal(plane1[:, :H], k1_sc_g[:])
+        place_odd_rows(plane1, [nc.sync, nc.scalar, nc.sync])
 
         k1_w_g = tile("k1_w_g", [P, H], U32)
         xq = tile("xq", [P, S], U32, tag="xq")
         nc.vector.tensor_copy(k1_w_g[:], d_w[:].indirect(k1_t[:]))
         nc.vector.tensor_copy(xq[:], x_w[:].indirect(offs_t[:]))
         w1 = tile("w1", [P, H], U32)
-        deal(w1[:].bitcast(I32), k1_w_g[:].bitcast(I32))
+        deal_words(w1[:], k1_w_g[:])
 
-        n3_t = load_list("n3_t", n3)
         gs_t = tile("gs_t", [P, PACK], F32)
-        nc.sync.dma_start(gs_t[:], gs.rearrange("(p t) o -> p (t o)", t=PACK))
+        nc.gpsimd.dma_start(gs_t[:], gs.rearrange("(p t) o -> p (t o)", t=PACK))
         k2_t = load_list("k2_t", k2)
         n6_t = load_list("n6_t", n6)
         n4_t = load_list("n4_t", n4)
@@ -140,7 +145,7 @@ def tile_picked_hcodeswapdpagmx_none_po_kernel(
         k2_w_g = tile("k2_w_g", [P, H], U32, tag="rb0")
         nc.vector.tensor_copy(k2_w_g[:], d_w[:].indirect(k2_t[:]))
         w2 = tile("w2", [P, H], U32)
-        deal(w2[:].bitcast(I32), k2_w_g[:].bitcast(I32))
+        deal_words(w2[:], k2_w_g[:])
 
         fetch_pair(2)
         fetch_pair(3)
@@ -148,11 +153,11 @@ def tile_picked_hcodeswapdpagmx_none_po_kernel(
         make_z(0, 1)
         put_pb(2)
         put_pb(3)
-        make_z(1, 0)
         put_rb(2)
-        put_rb(3)
+        make_z(1, 0)
         make_z(2, 0)
         make_z(2, 1)
+        put_rb(3)
         make_z(1, 1)
         make_z(3, 0)
         make_z(3, 1)
@@ -172,7 +177,10 @@ def tile_picked_hcodeswapdpagmx_none_po_kernel(
                     out=acc[:], lhsT=w2[:, cols].bitcast(FP8X4), lhsT_scale=plane2[:, cols],
                     rhs=zq[a][0][:].bitcast(FP8X4), rhs_scale=zq[a][1][:], start=True, stop=True,
                 )
-                nc.vector.tensor_scalar(h2[t][:, a * HALF : (a + 1) * HALF], acc[:], 0.0625, None, ALU.mult)
+                if t == 0:
+                    nc.scalar.activation(h2[t][:, a * HALF : (a + 1) * HALF], acc[:], COPY, scale=0.0625)
+                else:
+                    nc.vector.tensor_scalar(h2[t][:, a * HALF : (a + 1) * HALF], acc[:], 0.0625, None, ALU.mult)
 
         up = [tile(f"up{t}", [P, S], F32) for t in range(PACK)]
         dn = [tile(f"dn{t}", [P, S], F32) for t in range(PACK)]

@@ -18,7 +18,7 @@ COPY = mybir.ActivationFunctionType.Copy
 P = 128
 PACK = 4
 HALF = S // 2
-LIST_COLS = HALF // 16
+SPARE = 16
 
 
 def tile_picked_hcodeswapdpagmx_none_po_kernel(
@@ -40,7 +40,12 @@ def tile_picked_hcodeswapdpagmx_none_po_kernel(
         def load_scale_rows(name, src, width):
             t = tile(name, [P, width], U8)
             rows = src[0].bitcast(I32).unsqueeze(1).to_broadcast([16, 8, width // 4])
-            nc.sync.dma_start(t[:].bitcast(I32), rows)
+            nc.scalar.dma_start(t[:].bitcast(I32), rows)
+            return t
+
+        def window(name):
+            t = tile(name, [P, S + SPARE], F32)
+            nc.gpsimd.memset(t[:, S:], 0.0)
             return t
 
         def load_words(name, src, width):
@@ -60,10 +65,10 @@ def tile_picked_hcodeswapdpagmx_none_po_kernel(
         def deal(dst, src):
             nc.vector.tensor_copy(dst.rearrange("p (t m) -> p t m", t=PACK), src.rearrange("p (m t) -> p t m", t=PACK))
 
-        x_sc = load_scale_rows("x_sc", x_scales, T)
-        offs_t = load_list("offs_t", offs)
-        d_sc = load_scale_rows("d_sc", d_scales, G)
         k1_t = load_list("k1_t", k1)
+        d_sc = load_scale_rows("d_sc", d_scales, G)
+        offs_t = load_list("offs_t", offs)
+        x_sc = load_scale_rows("x_sc", x_scales, T)
         d_w = load_words("d_w", d_words, G)
         n2_t = load_list("n2_t", n2)
         n1_t = load_list("n1_t", n1)
@@ -72,19 +77,21 @@ def tile_picked_hcodeswapdpagmx_none_po_kernel(
 
         k1_sc_g = tile("k1_sc_g", [P, H], U8)
         x_sc_g = tile("x_sc_g", [P, S], U8)
-        nc.vector.tensor_copy(x_sc_g[:], x_sc[:].indirect(offs_t[:]))
         nc.vector.tensor_copy(k1_sc_g[:], d_sc[:].indirect(k1_t[:]))
+        nc.vector.tensor_copy(x_sc_g[:], x_sc[:].indirect(offs_t[:]))
         plane1 = tile("plane1", [P, H + S], U8)
-        nc.vector.tensor_copy(plane1[:, H:].bitcast(I32), x_sc_g[:].bitcast(I32))
         deal(plane1[:, :H], k1_sc_g[:])
+        nc.vector.tensor_copy(plane1[:, H:].bitcast(I32), x_sc_g[:].bitcast(I32))
         place_odd_rows(plane1, [nc.sync, nc.scalar, nc.sync])
 
         k1_w_g = tile("k1_w_g", [P, H], U32)
         xq = tile("xq", [P, S], U32, tag="xq")
         nc.vector.tensor_copy(k1_w_g[:], d_w[:].indirect(k1_t[:]))
+        k1_dealt = k1_w_g[:].bitcast(I32).rearrange("p (m t) -> p m t", t=PACK)
         nc.vector.tensor_copy(xq[:], x_w[:].indirect(offs_t[:]))
-        w1 = tile("w1", [P, H], U32)
-        deal_words(w1[:], k1_w_g[:])
+        w1 = tile("w1", [P, H], U32, tag="x_w")
+        nc.vector.tensor_copy(w1[:, :P].bitcast(I32), k1_dealt[:, :, 0])
+        nc.vector.tensor_copy(w1[:, P:].bitcast(I32).rearrange("p (t m) -> p m t", t=PACK - 1), k1_dealt[:, :, 1:])
 
         gs_t = tile("gs_t", [P, PACK], F32)
         nc.gpsimd.dma_start(gs_t[:], gs.rearrange("(p t) o -> p (t o)", t=PACK))
@@ -108,7 +115,7 @@ def tile_picked_hcodeswapdpagmx_none_po_kernel(
         pa = [tile(f"pa{t}", [P, W], F32) for t in range(PACK)]
         pb = [tile(f"pb{t}", [P, W], F32) for t in range(PACK)]
         rb = [tile(f"rb{t}", [P, W], F32) for t in range(PACK)]
-        dt = [tile(f"dt{t}", [P, S], F32) for t in range(PACK)]
+        dt = [window(f"dt{t}") for t in range(PACK)]
         zb = [tile(f"zb{a}", [P, HALF, PACK], BF16) for a in range(2)]
 
         def fetch_pair(t):
@@ -122,13 +129,29 @@ def tile_picked_hcodeswapdpagmx_none_po_kernel(
         def put_rb(t):
             nc.scalar.activation(dt[t][:].indirect(n2_t[:]), rb[t][:], COPY)
 
-        def make_z(t, a):
-            cols = slice(a * HALF, (a + 1) * HALF)
-            g = tile(f"g3_{t}_{a}", [P, HALF], F32)
-            m = tile(f"m_{t}_{a}", [P, HALF], F32)
-            nc.scalar.activation(g[:], dt[t][:].indirect(n3_t[:, a * LIST_COLS : (a + 1) * LIST_COLS]), COPY)
-            nc.vector.scalar_tensor_tensor(m[:], g[:], 0.5, dt[t][:, cols], ALU.mult, ALU.max)
-            nc.vector.tensor_scalar(zb[a][:, :, t], m[:], gs_t[:, t : t + 1], None, ALU.mult)
+        looked = {}
+        larger = {}
+
+        def fetch_n3(t, first, last, tag=None):
+            lo, hi = first * HALF, (last + 1) * HALF
+            looked[t, first] = tile(f"g3_{t}_{first}", [P, hi - lo], F32, tag=tag)
+            nc.scalar.activation(looked[t, first][:], dt[t][:].indirect(n3_t[:, lo // 16 : hi // 16]), COPY)
+
+        def take_larger(t, first, last):
+            lo, hi = first * HALF, (last + 1) * HALF
+            m = tile(f"m_{t}_{first}", [P, hi - lo], F32)
+            nc.vector.scalar_tensor_tensor(m[:], looked[t, first][:], 0.5, dt[t][:, lo:hi], ALU.mult, ALU.max)
+            for a in range(first, last + 1):
+                larger[t, a] = m[:, a * HALF - lo : (a + 1) * HALF - lo]
+
+        def weigh(t, a):
+            nc.vector.tensor_scalar(zb[a][:, :, t], larger[t, a], gs_t[:, t : t + 1], None, ALU.mult)
+
+        def make_z(t, first, last):
+            fetch_n3(t, first, last)
+            take_larger(t, first, last)
+            for a in range(first, last + 1):
+                weigh(t, a)
 
         fetch_pair(0)
         fetch_pair(1)
@@ -149,38 +172,47 @@ def tile_picked_hcodeswapdpagmx_none_po_kernel(
 
         fetch_pair(2)
         fetch_pair(3)
-        make_z(0, 0)
-        make_z(0, 1)
+        make_z(0, 0, 0)
         put_pb(2)
-        put_pb(3)
+        make_z(1, 0, 1)
         put_rb(2)
-        make_z(1, 0)
-        make_z(2, 0)
-        make_z(2, 1)
+        put_pb(3)
+        make_z(2, 0, 1)
         put_rb(3)
-        make_z(1, 1)
-        make_z(3, 0)
-        make_z(3, 1)
+        fetch_n3(0, 1, 1, tag="pb3")
+        fetch_n3(3, 0, 0)
+        fetch_n3(3, 1, 1)
+        take_larger(0, 1, 1)
+        take_larger(3, 0, 0)
+        weigh(0, 1)
+        take_larger(3, 1, 1)
+        weigh(3, 0)
+        weigh(3, 1)
 
-        h2 = [tile(f"h2_{t}", [P, S], F32) for t in range(PACK)]
-        zq = []
+        h2 = [window(f"h2_{t}") for t in range(PACK)]
+        zq = tile("zq", [P, S], U32)
+        zs = tile("zs", [P, S], U8)
+        halves = [slice(a * HALF, (a + 1) * HALF) for a in range(2)]
         for a in range(2):
-            codes = tile(f"zq{a}", [P, HALF], U32)
-            plane = tile(f"zs{a}", [P, HALF], U8)
-            nc.vector.quantize_mx(out=codes[:].bitcast(FP8X4), scales=plane[:], in_=zb[a][:].rearrange("p n t -> p (n t)"))
-            zq.append((codes, plane))
-        for t in range(PACK):
-            for a in range(2):
-                acc = psum.tile([P, HALF], F32, name=f"acc2_{t}_{a}", tag=f"bank{(t + PACK * (1 - a))}")
-                cols = slice(t * P, (t + 1) * P)
-                nc.tensor.matmul_mx(
-                    out=acc[:], lhsT=w2[:, cols].bitcast(FP8X4), lhsT_scale=plane2[:, cols],
-                    rhs=zq[a][0][:].bitcast(FP8X4), rhs_scale=zq[a][1][:], start=True, stop=True,
-                )
-                if t == 0:
-                    nc.scalar.activation(h2[t][:, a * HALF : (a + 1) * HALF], acc[:], COPY, scale=0.0625)
-                else:
-                    nc.vector.tensor_scalar(h2[t][:, a * HALF : (a + 1) * HALF], acc[:], 0.0625, None, ALU.mult)
+            nc.vector.quantize_mx(
+                out=zq[:, halves[a]].bitcast(FP8X4), scales=zs[:, halves[a]], in_=zb[a][:].rearrange("p n t -> p (n t)")
+            )
+
+        def second_product(t, part, bank):
+            acc = psum.tile([P, part.stop - part.start], F32, name=f"acc2_{bank}", tag=f"bank{bank}")
+            cols = slice(t * P, (t + 1) * P)
+            nc.tensor.matmul_mx(
+                out=acc[:], lhsT=w2[:, cols].bitcast(FP8X4), lhsT_scale=plane2[:, cols],
+                rhs=zq[:, part].bitcast(FP8X4), rhs_scale=zs[:, part], start=True, stop=True,
+            )
+            return acc
+
+        for a in range(2):
+            acc = second_product(0, halves[a], PACK * (1 - a))
+            nc.scalar.activation(h2[0][:, halves[a]], acc[:], COPY, scale=0.0625)
+        for t in range(1, PACK):
+            acc = second_product(t, slice(0, S), t)
+            nc.vector.tensor_scalar(h2[t][:, :S], acc[:], 0.0625, None, ALU.mult)
 
         up = [tile(f"up{t}", [P, S], F32) for t in range(PACK)]
         dn = [tile(f"dn{t}", [P, S], F32) for t in range(PACK)]
@@ -190,12 +222,9 @@ def tile_picked_hcodeswapdpagmx_none_po_kernel(
 
         def fetch_other(t):
             g = tile(f"g6_{t}", [P, S], F32)
-            for a in range(2):
-                nc.scalar.activation(
-                    g[:, a * HALF : (a + 1) * HALF], h2[t][:].indirect(n6_t[:, a * LIST_COLS : (a + 1) * LIST_COLS]), COPY
-                )
-            nc.vector.tensor_tensor(up[t][:], h2[t][:], g[:], ALU.max)
-            nc.vector.tensor_tensor(dn[t][:], h2[t][:], g[:], ALU.min)
+            nc.scalar.activation(g[:], h2[t][:].indirect(n6_t[:]), COPY)
+            nc.vector.tensor_tensor(up[t][:], h2[t][:, :S], g[:], ALU.max)
+            nc.vector.tensor_tensor(dn[t][:], h2[t][:, :S], g[:], ALU.min)
 
         def put_up(t):
             nc.scalar.activation(page[t][:].indirect(n4_t[:]), up[t][:], COPY)
@@ -208,13 +237,13 @@ def tile_picked_hcodeswapdpagmx_none_po_kernel(
 
         fetch_other(0)
         fetch_other(1)
-        put_up(0)
         fetch_other(2)
+        put_up(0)
+        fetch_other(3)
         put_dn(0)
         put_up(1)
-        fetch_other(3)
-        put_dn(1)
         put_up(2)
+        put_dn(1)
         put_up(3)
         put_dn(2)
         put_dn(3)

@@ -17,8 +17,14 @@ COPY = mybir.ActivationFunctionType.Copy
 
 P = 128
 PACK = 4
-HALF = S // 2
+QUADRANT = 32
+BLOCKS = K // 32
+COPIES = P // BLOCKS
+ENTRIES = 16
 SPARE = 16
+SIXTEENTH = 0.0625
+LAST = PACK - 1
+PIECES = [(0, 128), (128, 192), (192, 256)]
 
 
 def tile_picked_hcodeswapdpagmx_none_po_kernel(
@@ -33,65 +39,73 @@ def tile_picked_hcodeswapdpagmx_none_po_kernel(
             return sb.tile(shape, dtype, name=name, tag=tag or name, align_bytes=64)
 
         def load_list(name, src):
-            t = sb.tile(list(src.shape), U16, name=name)
-            nc.sync.dma_start(t[:], src)
-            return t
+            offsets = sb.tile(list(src.shape), U16, name=name)
+            nc.sync.dma_start(offsets[:], src)
+            return offsets
 
-        def load_scale_rows(name, src, width):
-            t = tile(name, [P, width], U8)
-            rows = src[0].bitcast(I32).unsqueeze(1).to_broadcast([16, 8, width // 4])
-            nc.scalar.dma_start(t[:].bitcast(I32), rows)
-            return t
+        def load_scale_table(name, src, width):
+            table = tile(name, [P, width], U8)
+            rows = src[0].bitcast(I32).unsqueeze(1).to_broadcast([BLOCKS, COPIES, width // 4])
+            nc.scalar.dma_start(table[:].bitcast(I32), rows)
+            return table
 
-        def window(name):
-            t = tile(name, [P, S + SPARE], F32)
-            nc.gpsimd.memset(t[:, S:], 0.0)
-            return t
+        def load_word_table(name, src, width):
+            table = tile(name, [P, width], U32)
+            nc.sync.dma_start(table[:].bitcast(I32), src[0].rearrange("p n t -> p (n t)").bitcast(I32))
+            return table
 
-        def load_words(name, src, width):
-            t = tile(name, [P, width], U32)
-            nc.sync.dma_start(t[:].bitcast(I32), src[0].rearrange("p n t -> p (n t)").bitcast(I32))
-            return t
+        def row_window(name):
+            window = tile(name, [P, S + SPARE], F32)
+            nc.gpsimd.memset(window[:, S:], 0.0)
+            return window
 
-        def place_odd_rows(plane, queues):
-            for r in range(1, 4):
-                queues[r - 1].dma_start(plane[r:P:32, :].bitcast(I32), plane[8 * r : P : 32, :].bitcast(I32))
-
-        def deal_words(dst, src):
-            nc.vector.tensor_copy(
-                dst.bitcast(I32).rearrange("p (t m) -> p m t", t=PACK), src.bitcast(I32).rearrange("p (m t) -> p m t", t=PACK)
-            )
-
-        def deal(dst, src):
+        def deal_bytes(dst, src):
             nc.vector.tensor_copy(dst.rearrange("p (t m) -> p t m", t=PACK), src.rearrange("p (m t) -> p t m", t=PACK))
 
+        def place_scale_rows(plane, queues):
+            for r in range(1, PACK):
+                dst = plane[r:P:QUADRANT, :].bitcast(I32)
+                queues[r - 1].dma_start(dst, plane[COPIES * r : P : QUADRANT, :].bitcast(I32))
+
+        def product(acc, words, plane, t, moving_words, moving_plane):
+            cols = slice(t * P, (t + 1) * P)
+            nc.tensor.matmul_mx(
+                out=acc,
+                lhsT=words[:, cols].bitcast(FP8X4),
+                lhsT_scale=plane[:, cols],
+                rhs=moving_words.bitcast(FP8X4),
+                rhs_scale=moving_plane,
+                start=True,
+                stop=True,
+            )
+
         k1_t = load_list("k1_t", k1)
-        d_sc = load_scale_rows("d_sc", d_scales, G)
+        d_sc = load_scale_table("d_sc", d_scales, G)
         offs_t = load_list("offs_t", offs)
-        x_sc = load_scale_rows("x_sc", x_scales, T)
-        d_w = load_words("d_w", d_words, G)
+        x_sc = load_scale_table("x_sc", x_scales, T)
+        d_w = load_word_table("d_w", d_words, G)
         n2_t = load_list("n2_t", n2)
         n1_t = load_list("n1_t", n1)
         n3_t = load_list("n3_t", n3)
-        x_w = load_words("x_w", x_words, T)
+        x_w = load_word_table("x_w", x_words, T)
 
-        k1_sc_g = tile("k1_sc_g", [P, H], U8)
-        x_sc_g = tile("x_sc_g", [P, S], U8)
-        nc.vector.tensor_copy(k1_sc_g[:], d_sc[:].indirect(k1_t[:]))
-        nc.vector.tensor_copy(x_sc_g[:], x_sc[:].indirect(offs_t[:]))
+        k1_bytes = tile("k1_bytes", [P, H], U8)
+        x_bytes = tile("x_bytes", [P, S], U8)
+        nc.vector.tensor_copy(k1_bytes[:], d_sc[:].indirect(k1_t[:]))
+        nc.vector.tensor_copy(x_bytes[:], x_sc[:].indirect(offs_t[:]))
         plane1 = tile("plane1", [P, H + S], U8)
-        deal(plane1[:, :H], k1_sc_g[:])
-        nc.vector.tensor_copy(plane1[:, H:].bitcast(I32), x_sc_g[:].bitcast(I32))
-        place_odd_rows(plane1, [nc.sync, nc.scalar, nc.sync])
+        deal_bytes(plane1[:, :H], k1_bytes[:])
+        nc.vector.tensor_copy(plane1[:, H:].bitcast(I32), x_bytes[:].bitcast(I32))
+        place_scale_rows(plane1, [nc.sync, nc.scalar, nc.sync])
 
-        k1_w_g = tile("k1_w_g", [P, H], U32)
-        xq = tile("xq", [P, S], U32, tag="xq")
-        nc.vector.tensor_copy(k1_w_g[:], d_w[:].indirect(k1_t[:]))
-        k1_dealt = k1_w_g[:].bitcast(I32).rearrange("p (m t) -> p m t", t=PACK)
+        k1_words = tile("k1_words", [P, H], U32)
+        xq = tile("xq", [P, S], U32)
+        nc.vector.tensor_copy(k1_words[:], d_w[:].indirect(k1_t[:]))
         nc.vector.tensor_copy(xq[:], x_w[:].indirect(offs_t[:]))
+        k1_by_tile = k1_words[:].bitcast(I32).rearrange("p (m t) -> p m t", t=PACK)
         w1 = tile("w1", [P, H], U32, tag="x_w")
-        nc.vector.tensor_copy(w1[:, :P].bitcast(I32), k1_dealt[:, :, 0])
-        nc.vector.tensor_copy(w1[:, P:].bitcast(I32).rearrange("p (t m) -> p m t", t=PACK - 1), k1_dealt[:, :, 1:])
+        nc.vector.tensor_copy(w1[:, :P].bitcast(I32), k1_by_tile[:, :, 0])
+        nc.vector.tensor_copy(w1[:, P:].bitcast(I32).rearrange("p (t m) -> p m t", t=LAST), k1_by_tile[:, :, 1:])
 
         gs_t = tile("gs_t", [P, PACK], F32)
         nc.gpsimd.dma_start(gs_t[:], gs.rearrange("(p t) o -> p (t o)", t=PACK))
@@ -100,23 +114,20 @@ def tile_picked_hcodeswapdpagmx_none_po_kernel(
         n4_t = load_list("n4_t", n4)
         n5_t = load_list("n5_t", n5)
 
-        h = []
-        for t in range(PACK):
-            acc = psum.tile([P, S], F32, name=f"acc{t}", tag=f"bank{t}")
-            cols = slice(t * P, (t + 1) * P)
-            nc.tensor.matmul_mx(
-                out=acc[:], lhsT=w1[:, cols].bitcast(FP8X4), lhsT_scale=plane1[:, cols],
-                rhs=xq[:].bitcast(FP8X4), rhs_scale=plane1[:, H:], start=True, stop=True,
-            )
-            ht = tile(f"h{t}", [P, S], F32)
-            nc.vector.tensor_scalar(ht[:], acc[:], 0.0625, None, ALU.mult)
-            h.append(ht)
+        h = [tile(f"h{t}", [P, S], F32) for t in range(PACK)]
+        parts = [(0, 0, S // 2, PACK), (0, S // 2, S, 0)] + [(t, 0, S, t) for t in range(1, PACK)]
+        for t, lo, hi, bank in parts:
+            acc = psum.tile([P, hi - lo], F32, name=f"h_acc{bank}", tag=f"bank{bank}")
+            product(acc[:], w1, plane1, t, xq[:, lo:hi], plane1[:, H + lo : H + hi])
+            nc.vector.tensor_scalar(h[t][:, lo:hi], acc[:], SIXTEENTH, None, ALU.mult)
 
         pa = [tile(f"pa{t}", [P, W], F32) for t in range(PACK)]
         pb = [tile(f"pb{t}", [P, W], F32) for t in range(PACK)]
         rb = [tile(f"rb{t}", [P, W], F32) for t in range(PACK)]
-        dt = [window(f"dt{t}") for t in range(PACK)]
-        zb = [tile(f"zb{a}", [P, HALF, PACK], BF16) for a in range(2)]
+        dt = [row_window(f"dt{t}") for t in range(PACK)]
+        zb = [tile(f"zb{a}", [P, hi - lo, PACK], BF16) for a, (lo, hi) in enumerate(PIECES)]
+        dt_n3 = {}
+        larger = {}
 
         def fetch_pair(t):
             nc.scalar.activation(pb[t][:], h[t][:].indirect(n2_t[:]), COPY)
@@ -129,102 +140,91 @@ def tile_picked_hcodeswapdpagmx_none_po_kernel(
         def put_rb(t):
             nc.scalar.activation(dt[t][:].indirect(n2_t[:]), rb[t][:], COPY)
 
-        looked = {}
-        larger = {}
-
         def fetch_n3(t, first, last, tag=None):
-            lo, hi = first * HALF, (last + 1) * HALF
-            looked[t, first] = tile(f"g3_{t}_{first}", [P, hi - lo], F32, tag=tag)
-            nc.scalar.activation(looked[t, first][:], dt[t][:].indirect(n3_t[:, lo // 16 : hi // 16]), COPY)
+            lo, hi = PIECES[first][0], PIECES[last][1]
+            dt_n3[t, first] = tile(f"dt_n3_{t}_{first}", [P, hi - lo], F32, tag=tag)
+            nc.scalar.activation(dt_n3[t, first][:], dt[t][:].indirect(n3_t[:, lo // ENTRIES : hi // ENTRIES]), COPY)
 
         def take_larger(t, first, last):
-            lo, hi = first * HALF, (last + 1) * HALF
-            m = tile(f"m_{t}_{first}", [P, hi - lo], F32)
-            nc.vector.scalar_tensor_tensor(m[:], looked[t, first][:], 0.5, dt[t][:, lo:hi], ALU.mult, ALU.max)
+            lo, hi = PIECES[first][0], PIECES[last][1]
+            m = tile(f"larger_{t}_{first}", [P, hi - lo], F32)
+            nc.vector.scalar_tensor_tensor(m[:], dt_n3[t, first][:], 0.5, dt[t][:, lo:hi], ALU.mult, ALU.max)
             for a in range(first, last + 1):
-                larger[t, a] = m[:, a * HALF - lo : (a + 1) * HALF - lo]
+                larger[t, a] = m[:, PIECES[a][0] - lo : PIECES[a][1] - lo]
 
-        def weigh(t, a):
-            nc.vector.tensor_scalar(zb[a][:, :, t], larger[t, a], gs_t[:, t : t + 1], None, ALU.mult)
+        def weigh(t, first, last):
+            for a in range(first, last + 1):
+                nc.vector.tensor_scalar(zb[a][:, :, t], larger[t, a], gs_t[:, t : t + 1], None, ALU.mult)
 
-        def make_z(t, first, last):
-            fetch_n3(t, first, last)
+        def make_z(t, first, last, tag=None):
+            fetch_n3(t, first, last, tag)
             take_larger(t, first, last)
-            for a in range(first, last + 1):
-                weigh(t, a)
+            weigh(t, first, last)
 
-        fetch_pair(0)
-        fetch_pair(1)
-        put_pb(0)
-        put_pb(1)
-        put_rb(0)
-        put_rb(1)
+        for step in (fetch_pair, put_pb, put_rb):
+            step(0)
+            step(1)
 
-        k2_sc_g = tile("k2_sc_g", [P, H], U8, tag="pa0")
-        nc.vector.tensor_copy(k2_sc_g[:], d_sc[:].indirect(k2_t[:]))
+        k2_bytes = tile("k2_bytes", [P, H], U8, tag="pa0")
+        nc.vector.tensor_copy(k2_bytes[:], d_sc[:].indirect(k2_t[:]))
         plane2 = tile("plane2", [P, H], U8)
-        deal(plane2[:], k2_sc_g[:])
-        place_odd_rows(plane2, [nc.sync, nc.sync, nc.sync])
-        k2_w_g = tile("k2_w_g", [P, H], U32, tag="rb0")
-        nc.vector.tensor_copy(k2_w_g[:], d_w[:].indirect(k2_t[:]))
+        deal_bytes(plane2[:], k2_bytes[:])
+        place_scale_rows(plane2, [nc.sync, nc.sync, nc.sync])
+        k2_words = tile("k2_words", [P, H], U32, tag="rb0")
+        nc.vector.tensor_copy(k2_words[:], d_w[:].indirect(k2_t[:]))
         w2 = tile("w2", [P, H], U32)
-        deal_words(w2[:], k2_w_g[:])
+        nc.vector.tensor_copy(
+            w2[:].bitcast(I32).rearrange("p (t m) -> p m t", t=PACK),
+            k2_words[:].bitcast(I32).rearrange("p (m t) -> p m t", t=PACK),
+        )
 
         fetch_pair(2)
         fetch_pair(3)
         make_z(0, 0, 0)
         put_pb(2)
-        make_z(1, 0, 1)
+        make_z(1, 0, 2)
         put_rb(2)
         put_pb(3)
-        make_z(2, 0, 1)
+        make_z(2, 0, 2)
         put_rb(3)
-        fetch_n3(0, 1, 1, tag="pb3")
-        fetch_n3(3, 0, 0)
-        fetch_n3(3, 1, 1)
-        take_larger(0, 1, 1)
-        take_larger(3, 0, 0)
-        weigh(0, 1)
-        take_larger(3, 1, 1)
-        weigh(3, 0)
-        weigh(3, 1)
+        make_z(0, 1, 2, tag="pb3")
+        fetch_n3(3, 0, 1)
+        fetch_n3(3, 2, 2)
+        take_larger(3, 0, 1)
+        take_larger(3, 2, 2)
+        weigh(3, 0, 2)
 
-        h2 = [window(f"h2_{t}") for t in range(PACK)]
         zq = tile("zq", [P, S], U32)
         zs = tile("zs", [P, S], U8)
-        halves = [slice(a * HALF, (a + 1) * HALF) for a in range(2)]
-        for a in range(2):
+        for a, (lo, hi) in enumerate(PIECES):
             nc.vector.quantize_mx(
-                out=zq[:, halves[a]].bitcast(FP8X4), scales=zs[:, halves[a]], in_=zb[a][:].rearrange("p n t -> p (n t)")
+                out=zq[:, lo:hi].bitcast(FP8X4), scales=zs[:, lo:hi], in_=zb[a][:].rearrange("p n t -> p (n t)")
             )
 
-        def second_product(t, part, bank):
-            acc = psum.tile([P, part.stop - part.start], F32, name=f"acc2_{bank}", tag=f"bank{bank}")
-            cols = slice(t * P, (t + 1) * P)
-            nc.tensor.matmul_mx(
-                out=acc[:], lhsT=w2[:, cols].bitcast(FP8X4), lhsT_scale=plane2[:, cols],
-                rhs=zq[:, part].bitcast(FP8X4), rhs_scale=zs[:, part], start=True, stop=True,
-            )
-            return acc
-
-        for a in range(2):
-            acc = second_product(0, halves[a], PACK * (1 - a))
-            nc.scalar.activation(h2[0][:, halves[a]], acc[:], COPY, scale=0.0625)
+        h2 = [row_window(f"h2_{t}") for t in range(PACK)]
+        for bank, group in ((PACK, PIECES[:-1]), (0, PIECES[-1:])):
+            start, stop = group[0][0], group[-1][1]
+            acc = psum.tile([P, stop - start], F32, name=f"h2_acc{bank}", tag=f"bank{bank}")
+            for lo, hi in group:
+                product(acc[:, lo - start : hi - start], w2, plane2, 0, zq[:, lo:hi], zs[:, lo:hi])
+            nc.scalar.activation(h2[0][:, start:stop], acc[:], COPY, scale=SIXTEENTH)
         for t in range(1, PACK):
-            acc = second_product(t, slice(0, S), t)
-            nc.vector.tensor_scalar(h2[t][:, :S], acc[:], 0.0625, None, ALU.mult)
+            acc = psum.tile([P, S], F32, name=f"h2_acc{t}", tag=f"bank{t}")
+            product(acc[:], w2, plane2, t, zq[:], zs[:])
+            nc.vector.tensor_scalar(h2[t][:, :S], acc[:], SIXTEENTH, None, ALU.mult)
 
         up = [tile(f"up{t}", [P, S], F32) for t in range(PACK)]
         dn = [tile(f"dn{t}", [P, S], F32) for t in range(PACK)]
         page = [tile(f"page{t}", [P, U], F32) for t in range(PACK)]
+        halves = [slice(0, U // 2), slice(U // 2, U)]
         ob = [tile(f"ob{a}", [P, U // 2, PACK], BF16) for a in range(2)]
         out_rows = out_0.rearrange("(p t) c -> p t c", t=PACK)
 
-        def fetch_other(t):
-            g = tile(f"g6_{t}", [P, S], F32)
-            nc.scalar.activation(g[:], h2[t][:].indirect(n6_t[:]), COPY)
-            nc.vector.tensor_tensor(up[t][:], h2[t][:, :S], g[:], ALU.max)
-            nc.vector.tensor_tensor(dn[t][:], h2[t][:, :S], g[:], ALU.min)
+        def fetch_n6(t):
+            h2_n6 = tile(f"h2_n6_{t}", [P, S], F32)
+            nc.scalar.activation(h2_n6[:], h2[t][:].indirect(n6_t[:]), COPY)
+            nc.vector.tensor_tensor(up[t][:], h2[t][:, :S], h2_n6[:], ALU.max)
+            nc.vector.tensor_tensor(dn[t][:], h2[t][:, :S], h2_n6[:], ALU.min)
 
         def put_up(t):
             nc.scalar.activation(page[t][:].indirect(n4_t[:]), up[t][:], COPY)
@@ -233,13 +233,13 @@ def tile_picked_hcodeswapdpagmx_none_po_kernel(
             nc.scalar.activation(page[t][:].indirect(n5_t[:]), dn[t][:], COPY)
             nc.sync.dma_start(out_rows[:, t, :], page[t][:])
             for a in range(2):
-                nc.vector.tensor_copy(ob[a][:, :, t], page[t][:, a * (U // 2) : (a + 1) * (U // 2)])
+                nc.vector.tensor_copy(ob[a][:, :, t], page[t][:, halves[a]])
 
-        fetch_other(0)
-        fetch_other(1)
-        fetch_other(2)
+        fetch_n6(0)
+        fetch_n6(1)
+        fetch_n6(2)
         put_up(0)
-        fetch_other(3)
+        fetch_n6(3)
         put_dn(0)
         put_up(1)
         put_up(2)
@@ -248,13 +248,17 @@ def tile_picked_hcodeswapdpagmx_none_po_kernel(
         put_dn(2)
         put_dn(3)
 
-        o_plane = tile("o_plane", [P, U], U8)
+        out_plane = tile("out_plane", [P, U], U8)
         words_out = out_1[0].rearrange("p n t -> p (n t)").bitcast(I32)
         for a in range(2):
-            cols = slice(a * (U // 2), (a + 1) * (U // 2))
-            codes = tile(f"oq{a}", [P, U // 2], U32)
-            nc.vector.quantize_mx(out=codes[:].bitcast(FP8X4), scales=o_plane[:, cols], in_=ob[a][:].rearrange("p n t -> p (n t)"))
-            nc.sync.dma_start(words_out[:, cols], codes[:].bitcast(I32))
-        for q in range(4):
+            codes = tile(f"out_codes{a}", [P, U // 2], U32)
+            nc.vector.quantize_mx(
+                out=codes[:].bitcast(FP8X4),
+                scales=out_plane[:, halves[a]],
+                in_=ob[a][:].rearrange("p n t -> p (n t)"),
+            )
+            nc.sync.dma_start(words_out[:, halves[a]], codes[:].bitcast(I32))
+        for q in range(P // QUADRANT):
             queue = nc.scalar if q % 2 == 0 else nc.sync
-            queue.dma_start(out_2[0, 4 * q : 4 * q + 4, :].bitcast(I32), o_plane[32 * q : 32 * q + 4, :].bitcast(I32))
+            live_rows = out_plane[QUADRANT * q : QUADRANT * q + PACK, :].bitcast(I32)
+            queue.dma_start(out_2[0, PACK * q : PACK * (q + 1), :].bitcast(I32), live_rows)

@@ -25,6 +25,8 @@ SPARE = 16
 SIXTEENTH = 0.0625
 LAST = PACK - 1
 PIECES = [(0, 128), (128, 192), (192, 256)]
+OUT_PIECES = [(0, 128), (128, 256), (256, 512)]
+VECTOR_COLS = 320
 
 
 def tile_picked_hcodeswapdpagmx_none_po_kernel(
@@ -208,7 +210,7 @@ def tile_picked_hcodeswapdpagmx_none_po_kernel(
             for lo, hi in group:
                 product(acc[:, lo - start : hi - start], w2, plane2, 0, zq[:, lo:hi], zs[:, lo:hi])
             nc.scalar.activation(h2[0][:, start:stop], acc[:], COPY, scale=SIXTEENTH)
-        for t in range(1, PACK):
+        for t in (2, 3, 1):
             acc = psum.tile([P, S], F32, name=f"h2_acc{t}", tag=f"bank{t}")
             product(acc[:], w2, plane2, t, zq[:], zs[:])
             nc.vector.tensor_scalar(h2[t][:, :S], acc[:], SIXTEENTH, None, ALU.mult)
@@ -216,8 +218,7 @@ def tile_picked_hcodeswapdpagmx_none_po_kernel(
         up = [tile(f"up{t}", [P, S], F32) for t in range(PACK)]
         dn = [tile(f"dn{t}", [P, S], F32) for t in range(PACK)]
         page = [tile(f"page{t}", [P, U], F32) for t in range(PACK)]
-        halves = [slice(0, U // 2), slice(U // 2, U)]
-        ob = [tile(f"ob{a}", [P, U // 2, PACK], BF16) for a in range(2)]
+        ob = [tile(f"ob{a}", [P, hi - lo, PACK], BF16) for a, (lo, hi) in enumerate(OUT_PIECES)]
         out_rows = out_0.rearrange("(p t) c -> p t c", t=PACK)
 
         def fetch_n6(t):
@@ -229,35 +230,39 @@ def tile_picked_hcodeswapdpagmx_none_po_kernel(
         def put_up(t):
             nc.scalar.activation(page[t][:].indirect(n4_t[:]), up[t][:], COPY)
 
-        def put_dn(t):
+        def put_dn(t, vector_cols=U):
             nc.scalar.activation(page[t][:].indirect(n5_t[:]), dn[t][:], COPY)
             nc.sync.dma_start(out_rows[:, t, :], page[t][:])
-            for a in range(2):
-                nc.vector.tensor_copy(ob[a][:, :, t], page[t][:, halves[a]])
+            for a, (lo, hi) in enumerate(OUT_PIECES):
+                cut = min(hi, vector_cols)
+                nc.vector.tensor_copy(ob[a][:, : cut - lo, t], page[t][:, lo:cut])
+                if cut < hi:
+                    nc.scalar.copy(ob[a][:, cut - lo :, t], page[t][:, cut:hi])
 
         fetch_n6(0)
-        fetch_n6(1)
         fetch_n6(2)
-        put_up(0)
         fetch_n6(3)
-        put_dn(0)
-        put_up(1)
+        put_up(0)
         put_up(2)
-        put_dn(1)
-        put_up(3)
+        put_dn(0)
+        fetch_n6(1)
         put_dn(2)
+        put_up(3)
+        put_up(1)
         put_dn(3)
+        put_dn(1, vector_cols=VECTOR_COLS)
 
         out_plane = tile("out_plane", [P, U], U8)
+        out_codes = tile("out_codes", [P, U], U32)
         words_out = out_1[0].rearrange("p n t -> p (n t)").bitcast(I32)
-        for a in range(2):
-            codes = tile(f"out_codes{a}", [P, U // 2], U32)
+        for a, (lo, hi) in enumerate(OUT_PIECES):
             nc.vector.quantize_mx(
-                out=codes[:].bitcast(FP8X4),
-                scales=out_plane[:, halves[a]],
+                out=out_codes[:, lo:hi].bitcast(FP8X4),
+                scales=out_plane[:, lo:hi],
                 in_=ob[a][:].rearrange("p n t -> p (n t)"),
             )
-            nc.sync.dma_start(words_out[:, halves[a]], codes[:].bitcast(I32))
+        for half in (slice(0, U // 2), slice(U // 2, U)):
+            nc.sync.dma_start(words_out[:, half], out_codes[:, half].bitcast(I32))
         for q in range(P // QUADRANT):
             queue = nc.scalar if q % 2 == 0 else nc.sync
             live_rows = out_plane[QUADRANT * q : QUADRANT * q + PACK, :].bitcast(I32)

from contextlib import ExitStack

import concourse.mybir as mybir

K, T, S, G, H, W, U = 512, 1024, 256, 2048, 512, 128, 512
FLOPS = 2 * 2 * K * H * S

F32 = mybir.dt.float32
BF16 = mybir.dt.bfloat16
I32 = mybir.dt.int32
U32 = mybir.dt.uint32
U16 = mybir.dt.uint16
U8 = mybir.dt.uint8
FP8X4 = mybir.dt.float8_e4m3fn_x4
ALU = mybir.AluOpType
COPY = mybir.ActivationFunctionType.Copy

P = 128
PACK = 4
QUADRANT = 32
BLOCKS = K // 32
COPIES = P // BLOCKS
ENTRIES = 16
SPARE = 16
SIXTEENTH = 0.0625
LAST = PACK - 1
PIECES = [(0, 128), (128, 192), (192, 256)]
OUT_PIECES = [(0, 128), (128, 256), (256, 512)]
VECTOR_COLS = 320


def tile_picked_hcodeswapdpagmx_none_po_kernel(
    tc, x_words, x_scales, d_words, d_scales, gs, offs, k1, n1, n2, n3, k2, n4, n5, n6, out_0, out_1, out_2
):
    nc = tc.nc
    with ExitStack() as ctx:
        sb = ctx.enter_context(tc.tile_pool(name="sb", bufs=1))
        psum = ctx.enter_context(tc.psum_pool(name="psum", bufs=1))

        def tile(name, shape, dtype, tag=None):
            return sb.tile(shape, dtype, name=name, tag=tag or name, align_bytes=64)

        def load_list(name, src):
            offsets = sb.tile(list(src.shape), U16, name=name)
            nc.sync.dma_start(offsets[:], src)
            return offsets

        def load_scale_table(name, src, width):
            table = tile(name, [P, width], U8)
            rows = src[0].bitcast(I32).unsqueeze(1).to_broadcast([BLOCKS, COPIES, width // 4])
            nc.scalar.dma_start(table[:].bitcast(I32), rows)
            return table

        def load_word_table(name, src, width):
            table = tile(name, [P, width], U32)
            nc.sync.dma_start(table[:].bitcast(I32), src[0].rearrange("p n t -> p (n t)").bitcast(I32))
            return table

        def row_window(name):
            window = tile(name, [P, S + SPARE], F32)
            nc.gpsimd.memset(window[:, S:], 0.0)
            return window

        def deal_bytes(dst, src):
            nc.vector.tensor_copy(dst.rearrange("p (t m) -> p t m", t=PACK), src.rearrange("p (m t) -> p t m", t=PACK))

        def place_scale_rows(plane, queues):
            for r in range(1, PACK):
                dst = plane[r:P:QUADRANT, :].bitcast(I32)
                queues[r - 1].dma_start(dst, plane[COPIES * r : P : QUADRANT, :].bitcast(I32))

        def product(acc, words, plane, t, moving_words, moving_plane):
            cols = slice(t * P, (t + 1) * P)
            nc.tensor.matmul_mx(
                out=acc,
                lhsT=words[:, cols].bitcast(FP8X4),
                lhsT_scale=plane[:, cols],
                rhs=moving_words.bitcast(FP8X4),
                rhs_scale=moving_plane,
                start=True,
                stop=True,
            )

        k1_t = load_list("k1_t", k1)
        d_sc = load_scale_table("d_sc", d_scales, G)
        offs_t = load_list("offs_t", offs)
        x_sc = load_scale_table("x_sc", x_scales, T)
        d_w = load_word_table("d_w", d_words, G)
        n2_t = load_list("n2_t", n2)
        n1_t = load_list("n1_t", n1)
        n3_t = load_list("n3_t", n3)
        x_w = load_word_table("x_w", x_words, T)

        k1_bytes = tile("k1_bytes", [P, H], U8)
        x_bytes = tile("x_bytes", [P, S], U8)
        nc.vector.tensor_copy(k1_bytes[:], d_sc[:].indirect(k1_t[:]))
        nc.vector.tensor_copy(x_bytes[:], x_sc[:].indirect(offs_t[:]))
        plane1 = tile("plane1", [P, H + S], U8)
        deal_bytes(plane1[:, :H], k1_bytes[:])
        nc.vector.tensor_copy(plane1[:, H:].bitcast(I32), x_bytes[:].bitcast(I32))
        place_scale_rows(plane1, [nc.sync, nc.scalar, nc.sync])

        k1_words = tile("k1_words", [P, H], U32)
        xq = tile("xq", [P, S], U32)
        nc.vector.tensor_copy(k1_words[:], d_w[:].indirect(k1_t[:]))
        nc.vector.tensor_copy(xq[:], x_w[:].indirect(offs_t[:]))
        k1_by_tile = k1_words[:].bitcast(I32).rearrange("p (m t) -> p m t", t=PACK)
        w1 = tile("w1", [P, H], U32, tag="x_w")
        nc.vector.tensor_copy(w1[:, :P].bitcast(I32), k1_by_tile[:, :, 0])
        nc.vector.tensor_copy(w1[:, P:].bitcast(I32).rearrange("p (t m) -> p m t", t=LAST), k1_by_tile[:, :, 1:])

        gs_t = tile("gs_t", [P, PACK], F32)
        nc.gpsimd.dma_start(gs_t[:], gs.rearrange("(p t) o -> p (t o)", t=PACK))
        k2_t = load_list("k2_t", k2)
        n6_t = load_list("n6_t", n6)
        n4_t = load_list("n4_t", n4)
        n5_t = load_list("n5_t", n5)

        h = [tile(f"h{t}", [P, S], F32) for t in range(PACK)]
        parts = [(0, 0, S // 2, PACK), (0, S // 2, S, 0)] + [(t, 0, S, t) for t in range(1, PACK)]
        for t, lo, hi, bank in parts:
            acc = psum.tile([P, hi - lo], F32, name=f"h_acc{bank}", tag=f"bank{bank}")
            product(acc[:], w1, plane1, t, xq[:, lo:hi], plane1[:, H + lo : H + hi])
            nc.vector.tensor_scalar(h[t][:, lo:hi], acc[:], SIXTEENTH, None, ALU.mult)

        pa = [tile(f"pa{t}", [P, W], F32) for t in range(PACK)]
        pb = [tile(f"pb{t}", [P, W], F32) for t in range(PACK)]
        rb = [tile(f"rb{t}", [P, W], F32) for t in range(PACK)]
        dt = [row_window(f"dt{t}") for t in range(PACK)]
        zb = [tile(f"zb{a}", [P, hi - lo, PACK], BF16) for a, (lo, hi) in enumerate(PIECES)]
        dt_n3 = {}
        larger = {}

        def fetch_pair(t):
            nc.scalar.activation(pb[t][:], h[t][:].indirect(n2_t[:]), COPY)
            nc.scalar.activation(pa[t][:], h[t][:].indirect(n1_t[:]), COPY)
            nc.vector.tensor_tensor(rb[t][:], pa[t][:], pb[t][:], ALU.subtract)

        def put_pb(t):
            nc.scalar.activation(dt[t][:].indirect(n1_t[:]), pb[t][:], COPY)

        def put_rb(t):
            nc.scalar.activation(dt[t][:].indirect(n2_t[:]), rb[t][:], COPY)

        def fetch_n3(t, first, last, tag=None):
            lo, hi = PIECES[first][0], PIECES[last][1]
            dt_n3[t, first] = tile(f"dt_n3_{t}_{first}", [P, hi - lo], F32, tag=tag)
            nc.scalar.activation(dt_n3[t, first][:], dt[t][:].indirect(n3_t[:, lo // ENTRIES : hi // ENTRIES]), COPY)

        def take_larger(t, first, last):
            lo, hi = PIECES[first][0], PIECES[last][1]
            m = tile(f"larger_{t}_{first}", [P, hi - lo], F32)
            nc.vector.scalar_tensor_tensor(m[:], dt_n3[t, first][:], 0.5, dt[t][:, lo:hi], ALU.mult, ALU.max)
            for a in range(first, last + 1):
                larger[t, a] = m[:, PIECES[a][0] - lo : PIECES[a][1] - lo]

        def weigh(t, first, last):
            for a in range(first, last + 1):
                nc.vector.tensor_scalar(zb[a][:, :, t], larger[t, a], gs_t[:, t : t + 1], None, ALU.mult)

        def make_z(t, first, last, tag=None):
            fetch_n3(t, first, last, tag)
            take_larger(t, first, last)
            weigh(t, first, last)

        for step in (fetch_pair, put_pb, put_rb):
            step(0)
            step(1)

        k2_bytes = tile("k2_bytes", [P, H], U8, tag="pa0")
        nc.vector.tensor_copy(k2_bytes[:], d_sc[:].indirect(k2_t[:]))
        plane2 = tile("plane2", [P, H], U8)
        deal_bytes(plane2[:], k2_bytes[:])
        place_scale_rows(plane2, [nc.sync, nc.sync, nc.sync])
        k2_words = tile("k2_words", [P, H], U32, tag="rb0")
        nc.vector.tensor_copy(k2_words[:], d_w[:].indirect(k2_t[:]))
        w2 = tile("w2", [P, H], U32)
        nc.vector.tensor_copy(
            w2[:].bitcast(I32).rearrange("p (t m) -> p m t", t=PACK),
            k2_words[:].bitcast(I32).rearrange("p (m t) -> p m t", t=PACK),
        )

        fetch_pair(2)
        fetch_pair(3)
        make_z(0, 0, 0)
        put_pb(2)
        make_z(1, 0, 2)
        put_rb(2)
        put_pb(3)
        make_z(2, 0, 2)
        put_rb(3)
        make_z(0, 1, 2, tag="pb3")
        fetch_n3(3, 0, 1)
        fetch_n3(3, 2, 2)
        take_larger(3, 0, 1)
        take_larger(3, 2, 2)
        weigh(3, 0, 2)

        zq = tile("zq", [P, S], U32)
        zs = tile("zs", [P, S], U8)
        for a, (lo, hi) in enumerate(PIECES):
            nc.vector.quantize_mx(
                out=zq[:, lo:hi].bitcast(FP8X4), scales=zs[:, lo:hi], in_=zb[a][:].rearrange("p n t -> p (n t)")
            )

        h2 = [row_window(f"h2_{t}") for t in range(PACK)]
        for bank, group in ((PACK, PIECES[:-1]), (0, PIECES[-1:])):
            start, stop = group[0][0], group[-1][1]
            acc = psum.tile([P, stop - start], F32, name=f"h2_acc{bank}", tag=f"bank{bank}")
            for lo, hi in group:
                product(acc[:, lo - start : hi - start], w2, plane2, 0, zq[:, lo:hi], zs[:, lo:hi])
            nc.scalar.activation(h2[0][:, start:stop], acc[:], COPY, scale=SIXTEENTH)
        for t in (2, 3, 1):
            acc = psum.tile([P, S], F32, name=f"h2_acc{t}", tag=f"bank{t}")
            product(acc[:], w2, plane2, t, zq[:], zs[:])
            nc.vector.tensor_scalar(h2[t][:, :S], acc[:], SIXTEENTH, None, ALU.mult)

        up = [tile(f"up{t}", [P, S], F32) for t in range(PACK)]
        dn = [tile(f"dn{t}", [P, S], F32) for t in range(PACK)]
        page = [tile(f"page{t}", [P, U], F32) for t in range(PACK)]
        ob = [tile(f"ob{a}", [P, hi - lo, PACK], BF16) for a, (lo, hi) in enumerate(OUT_PIECES)]
        out_rows = out_0.rearrange("(p t) c -> p t c", t=PACK)

        def fetch_n6(t):
            h2_n6 = tile(f"h2_n6_{t}", [P, S], F32)
            nc.scalar.activation(h2_n6[:], h2[t][:].indirect(n6_t[:]), COPY)
            nc.vector.tensor_tensor(up[t][:], h2[t][:, :S], h2_n6[:], ALU.max)
            nc.vector.tensor_tensor(dn[t][:], h2[t][:, :S], h2_n6[:], ALU.min)

        def put_up(t):
            nc.scalar.activation(page[t][:].indirect(n4_t[:]), up[t][:], COPY)

        def put_dn(t, vector_cols=U):
            nc.scalar.activation(page[t][:].indirect(n5_t[:]), dn[t][:], COPY)
            nc.sync.dma_start(out_rows[:, t, :], page[t][:])
            for a, (lo, hi) in enumerate(OUT_PIECES):
                cut = min(hi, vector_cols)
                nc.vector.tensor_copy(ob[a][:, : cut - lo, t], page[t][:, lo:cut])
                if cut < hi:
                    nc.scalar.copy(ob[a][:, cut - lo :, t], page[t][:, cut:hi])

        fetch_n6(0)
        fetch_n6(2)
        fetch_n6(3)
        put_up(0)
        put_up(2)
        put_dn(0)
        fetch_n6(1)
        put_dn(2)
        put_up(3)
        put_up(1)
        put_dn(3)
        put_dn(1, vector_cols=VECTOR_COLS)

        out_plane = tile("out_plane", [P, U], U8)
        out_codes = tile("out_codes", [P, U], U32)
        words_out = out_1[0].rearrange("p n t -> p (n t)").bitcast(I32)
        for a, (lo, hi) in enumerate(OUT_PIECES):
            nc.vector.quantize_mx(
                out=out_codes[:, lo:hi].bitcast(FP8X4),
                scales=out_plane[:, lo:hi],
                in_=ob[a][:].rearrange("p n t -> p (n t)"),
            )
        for half in (slice(0, U // 2), slice(U // 2, U)):
            nc.sync.dma_start(words_out[:, half], out_codes[:, half].bitcast(I32))
        for q in range(P // QUADRANT):
            queue = nc.scalar if q % 2 == 0 else nc.sync
            live_rows = out_plane[QUADRANT * q : QUADRANT * q + PACK, :].bitcast(I32)
            queue.dma_start(out_2[0, PACK * q : PACK * (q + 1), :].bitcast(I32), live_rows)
